import numpy as np
import ml_dtypes


def mxq(x, axis, fmt="e4m3"):
    dtype, down = {"e4m3": (ml_dtypes.float8_e4m3fn, 7), "e5m2": (ml_dtypes.float8_e5m2, 14)}[fmt]
    v = np.moveaxis(np.asarray(x, np.float32).astype(ml_dtypes.bfloat16).astype(np.float64), axis, -1)
    blocks = v.reshape(v.shape[:-1] + (-1, 32))
    amax = np.abs(blocks).max(-1, keepdims=True)
    byte = np.maximum(np.where(amax > 0, np.frexp(amax)[1] - 1 + 127, 0) - down, 1)
    scale = np.exp2(byte - 127.0)
    codes = (blocks / scale).astype(np.float32).astype(dtype).astype(np.float64)
    return np.moveaxis((codes * scale).reshape(v.shape), -1, axis)


WIDE = False


def mx_kscale(k):
    if not WIDE:
        return np.ones(k)
    levels = np.array([10, -10, 5, -5, 0])
    if k % 512:
        return np.exp2(np.random.permutation(np.resize(levels, k // 32))).repeat(32)
    a = np.empty((k // 512, 16))
    for p in range(k // 512):
        a[p, :8] = np.random.permutation(np.resize(levels, 8))
        for g in range(8):
            far = levels[np.abs(levels - a[p, g]) >= 10]
            a[p, g + 8] = far[np.random.randint(len(far))]
    return np.exp2(a.ravel()).repeat(32)


def f64(x):
    return np.asarray(x).astype(np.float64)


def striped(idx):
    return np.tile(np.asarray(idx).reshape(-1, 16).T, (8, 1)).astype(np.uint16)


def unstriped(offs):
    return offs[:16].T.reshape(-1).astype(np.int64)


E2M1 = np.array([0.0, 0.5, 1.0, 1.5, 2.0, 3.0, 4.0, 6.0, -0.0, -0.5, -1.0, -1.5, -2.0, -3.0, -4.0, -6.0])


def pack_weight(w, fmt):
    k, n = w.shape
    w = f64(np.asarray(w, np.float32).astype(ml_dtypes.bfloat16)).reshape(k // 32, 32, n)
    amax = np.abs(w).max(1)
    if fmt == "e4m3":
        byte = np.frexp(amax)[1] - 1 + 127 - 7
    else:
        mant, ex = np.frexp(amax / 6.0)
        byte = np.where(mant > 0.5, ex, ex - 1) + 127
    byte = np.clip(np.where(amax > 0, byte, 1), 1, 254)
    scaled = (w * np.exp2(127.0 - byte)[:, None, :]).reshape(k, n).astype(np.float32)
    by_word = np.ascontiguousarray(scaled.reshape(k // 512, 128, 4, n).transpose(0, 1, 3, 2))
    if fmt == "e4m3":
        words = by_word.astype(ml_dtypes.float8_e4m3fn).view(np.uint8)
    else:
        c = by_word.astype(ml_dtypes.float4_e2m1fn).view(np.uint8) & 0xF
        words = (c[..., 0::2] | (c[..., 1::2] << 4)).reshape(k // 512, 128, 2 * n)
    return np.ascontiguousarray(words), np.ascontiguousarray(byte.astype(np.uint8).reshape(k // 512, 16, n))


def unpack_weight(words, scales, fmt):
    g, _, n = scales.shape
    words = np.ascontiguousarray(words).reshape(g, 128, n, -1)
    if fmt == "e4m3":
        vals = words.view(ml_dtypes.float8_e4m3fn).astype(np.float64)
    else:
        nib = np.empty((g, 128, n, 4), np.uint8)
        nib[..., 0::2] = words & 0xF
        nib[..., 1::2] = words >> 4
        vals = E2M1[nib]
    vals = vals * np.repeat(np.exp2(scales.astype(np.float64) - 127.0), 8, axis=1)[..., None]
    return vals.transpose(0, 1, 3, 2).reshape(g * 512, n)


def bf(x):
    return np.asarray(x, np.float32).astype(ml_dtypes.bfloat16)


def planes(Y):
    r, m = Y.shape
    b = f64(bf(Y)).reshape(r // 32, 32, m)
    amax = np.abs(b).max(1)
    byte = np.clip(np.where(amax > 0, np.frexp(amax)[1] - 1 + 127 - 7, 1), 1, 254)
    codes = (b * np.exp2(127.0 - byte)[:, None, :]).reshape(r, m).astype(np.float32).astype(ml_dtypes.float8_e4m3fn).view(np.uint8)
    words = codes.reshape(r // 512, 128, 4, m).transpose(0, 1, 3, 2)
    return np.ascontiguousarray(words), np.ascontiguousarray(byte.astype(np.uint8).reshape(r // 512, 16, m))


D, T, I, Q, E, U, G = 512, 2048, 512, 256, 512, 1024, 64


def setup_inputs():
    n = np.random.standard_normal
    idx = np.random.permutation(T)[:I]
    idx2 = np.random.permutation(U)[:I]
    fd = mx_kscale(D)
    fi = mx_kscale(I)
    ti = np.ones(T)
    ti[idx] = fi
    keysp = pack_weight(n((D, T)) / fd[:, None], "e2m1")
    return {
        "query": (n((D, Q)) * 0.9 / np.sqrt(D) * fd[:, None]).astype(np.float32),
        "keys_words": keysp[0],
        "keys_scales": keysp[1],
        "query2": (n((D, Q)) * 0.9 / np.sqrt(D) * fd[:, None]).astype(np.float32),
        "notes": (n((D, U)) / fd[:, None]).astype(np.float32),
        "lam": (np.random.uniform(0.1, 0.5, (Q, 1))).astype(np.float32),
        "shy": (np.random.uniform(20.0, 60.0, (Q, 1))).astype(np.float32),
        "os": (np.random.uniform(4.0, 16.0, (1, I)) * fi).astype(np.float32),
        "vals": (n((E, T)) / ti).astype(np.float32),
        "memq": (np.random.uniform(0.3, 1.0, (1, Q))).astype(np.float32),
        "offs": striped(idx),
        "offs2": striped(idx2),
    }


def reference(query, keys_words, keys_scales, query2, notes, lam, shy, os, vals, memq, offs, offs2):
    idx = unstriped(offs)
    idx2 = unstriped(offs2)
    keysu = unpack_weight(keys_words, keys_scales, "e2m1")
    queryq = mxq(f64(query), 0, "e4m3")
    keysidxg = keysu[:, idx]
    a = queryq.T @ keysidxg
    query2q = mxq(f64(query2), 0, "e4m3")
    notesidx2q = mxq(f64(notes)[:, idx2], 0, "e4m3")
    b = query2q.T @ notesidx2q
    s = np.maximum(a, b) + np.minimum(a, b) * f64(lam)
    p = np.exp(s - np.max(s, axis=1, keepdims=True))
    r = p / np.sum(p, axis=1, keepdims=True)
    pg = r.reshape(Q, G, I // G).sum(axis=2)
    k0 = np.exp(pg * f64(shy) * (-1.0))
    kr = np.repeat(k0, I // G, axis=1)
    u0 = r * kr
    w = u0 / np.sum(u0, axis=1, keepdims=True)
    wo1 = w * f64(os)
    wt1 = wo1.T
    vt1 = f64(vals)[:, idx].T
    vt1q = mxq(vt1, 0, "e4m3")
    wt1q = mxq(wt1, 0, "e4m3")
    o = vt1q.T @ wt1q
    o1 = np.pad(o, ((0, 0), (1, 0)))[:, :Q]
    y = o - o1 * f64(memq)
    words, scales = planes(y)
    return y, words, scales

@@ -1,0 +1,306 @@
+from contextlib import ExitStack
+
+import concourse.mybir as mybir
+from concourse.masks import make_identity
+
+F32 = mybir.dt.float32
+BF16 = mybir.dt.bfloat16
+I32 = mybir.dt.int32
+U32 = mybir.dt.uint32
+U16 = mybir.dt.uint16
+U8 = mybir.dt.uint8
+FP8X4 = mybir.dt.float8_e4m3fn_x4
+FP4X4 = mybir.dt.float4_e2m1fn_x4
+ALU = mybir.AluOpType
+ACT = mybir.ActivationFunctionType
+AXIS = mybir.AxisListType
+
+D, T, I, Q, E, U = 512, 2048, 512, 256, 512, 1024
+RUN = 8
+G = I // RUN
+P = 128
+PACK = 4
+QT = Q // P
+FLOPS = 2 * Q * I * D * 2 + 2 * E * Q * I
+
+
+def weave(engine_copy, dst, src):
+    engine_copy(out=dst.rearrange("p (c i) t -> p c t i", i=4), in_=src.rearrange("p t (c i) -> p c t i", i=4))
+
+
+def tile_attend_twopools_crowdshy_rowchanges_pl_kernel(
+    tc, query, keys_words, keys_scales, query2, notes, lam, shy, slot_factor, vals, memq, offs, offs2, out_0, out_1, out_2
+):
+    nc = tc.nc
+    with ExitStack() as ctx:
+        lists = ctx.enter_context(tc.tile_pool(name="lists", bufs=1))
+        sb = ctx.enter_context(tc.tile_pool(name="sb", bufs=1))
+        ps = ctx.enter_context(tc.psum_pool(name="ps", bufs=1))
+
+        def bank(n, shape, name):
+            return ps.tile(shape, F32, tag="bank%d" % n, name=name)
+
+        def quantize(codes, scales, woven):
+            nc.vector.quantize_mx(out=codes.bitcast(FP8X4), scales=scales, in_=woven.rearrange("p c t -> p (c t)"))
+
+        idx = lists.tile([P, I // 16], U16)
+        idx2 = lists.tile([P, I // 16], U16)
+
+        key_words = sb.tile([P, T], U16, align_bytes=64)
+        key_scales = sb.tile([P, T], U8, align_bytes=64)
+        q_raw = sb.tile([P, PACK, Q], F32)
+        q2_raw = sb.tile([P, PACK, Q], F32)
+        note_rows = [sb.tile([P, U], F32, name="note_rows%d" % t) for t in range(PACK)]
+        val_rows = [sb.tile([P, T], F32, name="val_rows%d" % j) for j in range(PACK)]
+        lam_c = sb.tile([P, QT], F32)
+        shy_c = sb.tile([P, QT], F32)
+        os_c = sb.tile([P, PACK], F32)
+        memq_c = sb.tile([P, QT], F32)
+        ident = sb.tile([P, P], F32)
+        carried = sb.tile([P, PACK, Q], F32)
+
+        nc.gpsimd.memset(key_scales[:].bitcast(I32), 0)
+        make_identity(nc, ident[:])
+        nc.vector.memset(carried[:, :, 0:1], 0.0)
+
+        with nc.allow_non_contiguous_dma(reason="one value a query row"):
+            nc.sync.dma_start(shy_c[:], shy.rearrange("(r p) o -> p (r o)", p=P))
+        nc.sync.dma_start(idx[:], offs)
+        nc.sync.dma_start(key_words[:].bitcast(I32), keys_words[0].bitcast(I32))
+        notes_planes = notes.rearrange("(p t) u -> t p u", t=PACK)
+        nc.sync.dma_start(note_rows[0][:], notes_planes[0])
+        scale_rows = keys_scales[0].bitcast(I32)
+        for quad in range(4):
+            nc.sync.dma_start(key_scales[32 * quad : 32 * quad + 4, :].bitcast(I32), scale_rows[4 * quad : 4 * quad + 4, :])
+        nc.sync.dma_start(idx2[:], offs2)
+        nc.sync.dma_start(note_rows[1][:], notes_planes[1])
+        nc.sync.dma_start(note_rows[2][:], notes_planes[2])
+        nc.sync.dma_start(os_c[:], slot_factor.rearrange("o (p c) -> p (o c)", p=P))
+        nc.sync.dma_start(note_rows[3][:], notes_planes[3])
+        nc.sync.dma_start(memq_c[:], memq.rearrange("o (p c) -> p (o c)", p=P))
+        nc.sync.dma_start(q_raw[:], query.rearrange("(p t) q -> p t q", t=PACK))
+        nc.sync.dma_start(q2_raw[:], query2.rearrange("(p t) q -> p t q", t=PACK))
+        with nc.allow_non_contiguous_dma(reason="one value a query row"):
+            nc.sync.dma_start(lam_c[:], lam.rearrange("(r p) o -> p (r o)", p=P))
+        vals_planes = vals.rearrange("(p j) t -> j p t", j=PACK)
+        for j in range(PACK):
+            nc.sync.dma_start(val_rows[j][:], vals_planes[j])
+
+        neg_shy = sb.tile([P, QT], F32)
+        nc.scalar.mul(neg_shy[:], shy_c[:], -1.0)
+
+        key_words_g = sb.tile([P, I], U16, align_bytes=64)
+        key_scales_g = sb.tile([P, I], U8, align_bytes=64)
+        nc.vector.tensor_copy(key_words_g[:], key_words[:].indirect(idx[:]))
+        nc.vector.tensor_copy(key_scales_g[:], key_scales[:].indirect(idx[:]))
+
+        notes_woven = sb.tile([P, I, PACK], BF16, align_bytes=64)
+        note_scales = sb.tile([P, I], U8, align_bytes=64)
+        notes_g = sb.tile([P, PACK, I], BF16)
+        half = I // 2
+        nc.scalar.activation(notes_g[:, 0, :], note_rows[0][:].indirect(idx2[:]), ACT.Copy)
+        nc.scalar.activation(notes_g[:, 1, :], note_rows[1][:].indirect(idx2[:]), ACT.Copy)
+        nc.vector.tensor_copy(notes_g[:, 2, :], note_rows[2][:].indirect(idx2[:]))
+        nc.vector.tensor_copy(notes_g[:, 3, :half], note_rows[3][:].indirect(idx2[:, : half // 16]))
+        nc.scalar.activation(notes_g[:, 3, half:], note_rows[3][:].indirect(idx2[:, half // 16 :]), ACT.Copy)
+        weave(nc.vector.tensor_copy, notes_woven[:], notes_g[:])
+
+        def quantized_queries(raw, r, name, codes_tag):
+            woven = sb.tile([P, P, PACK], BF16, align_bytes=64, name="%s_woven%d" % (name, r))
+            codes = sb.tile([P, P], U32, align_bytes=64, name="%s_codes%d" % (name, r), tag=codes_tag)
+            scales = sb.tile([P, P], U8, align_bytes=64, name="%s_scales%d" % (name, r))
+            weave(nc.scalar.copy, woven[:], raw[:, :, r * P : (r + 1) * P])
+            quantize(codes[:], scales[:], woven[:])
+            return codes, scales
+
+        a_ps, a_sb, b_ps = [], [], []
+        for r in range(QT):
+            codes, scales = quantized_queries(q_raw, r, "q", ("q_codes0", "q2_woven0")[r])
+            a_ps.append(bank(r, [P, I], "a_ps%d" % r))
+            nc.tensor.matmul_mx(
+                out=a_ps[r][:], lhsT=codes[:].bitcast(FP8X4), lhsT_scale=scales[:],
+                rhs=key_words_g[:].bitcast(FP4X4), rhs_scale=key_scales_g[:], start=True, stop=True,
+            )
+            if r == 0:
+                note_codes = sb.tile([P, I], U32, align_bytes=64, tag="q_woven0")
+                quantize(note_codes[:], note_scales[:], notes_woven[:])
+            codes, scales = quantized_queries(q2_raw, r, "q2", "q2_codes%d" % r)
+            b_ps.append(bank(2 + r, [P, I], "b_ps%d" % r))
+            nc.tensor.matmul_mx(
+                out=b_ps[r][:], lhsT=codes[:].bitcast(FP8X4), lhsT_scale=scales[:],
+                rhs=note_codes[:].bitcast(FP8X4), rhs_scale=note_scales[:], start=True, stop=True,
+            )
+        a_both = sb.tile([P, QT, I], F32, tag="q2_raw")
+        for r in range(QT):
+            a_sb.append(a_both[:, r, :])
+            nc.scalar.copy(a_sb[r], a_ps[r][:])
+
+        os_ps = bank(4, [P, PACK, P], "os_ps")
+        for c in range(PACK):
+            nc.tensor.transpose(os_ps[:, c, :], os_c[:, c : c + 1].to_broadcast([P, P]), ident[:])
+        memq_ps = bank(5, [P, QT, P], "memq_ps")
+        for c in range(QT):
+            nc.tensor.transpose(memq_ps[:, c, :], memq_c[:, c : c + 1].to_broadcast([P, P]), ident[:])
+        memq_row = sb.tile([P, Q], F32, tag="q2_codes1", align_bytes=64)
+        nc.scalar.copy(memq_row[:].rearrange("m (p c) -> m p c", c=QT), memq_ps[:].rearrange("m c p -> m p c"))
+
+        def turn(rows_bf16, bank_part):
+            words = rows_bf16.bitcast(F32)
+            for u in range(2):
+                nc.tensor.transpose(bank_part[:, u, :], words[:, u::2], ident[:])
+
+        def as_word_pairs(woven):
+            return woven.rearrange("p c t -> p (c t)").bitcast(F32).rearrange("p (c u) -> p c u", u=2)
+
+        def wide(name, r, dtype=F32):
+            return sb.tile([P, I], dtype, name="%s%d" % (name, r), align_bytes=64)
+
+        def small(name, r, width=1):
+            return sb.tile([P, width], F32, name="%s%d" % (name, r), align_bytes=64)
+
+        tiles = range(QT)
+        lo, hi, score, p, pos = ([wide(name, r) for r in tiles] for name in ("lo", "hi", "score", "p", "pos"))
+        w_rows = [wide("w_rows", r, BF16) for r in tiles]
+        neg_max, z, rz, slope, z2, rz2 = (
+            [small(name, r) for r in tiles] for name in ("neg_max", "z", "rz", "slope", "z2", "rz2")
+        )
+        run_sum, k0, damped = ([small(name, r, G) for r in tiles] for name in ("run_sum", "k0", "damped"))
+
+        def by_runs(ap):
+            return ap.rearrange("p (g m) -> p g m", m=RUN)
+
+        def smaller(r):
+            nc.vector.tensor_tensor(lo[r][:], b_ps[r][:], a_sb[r], ALU.min)
+
+        def larger(r):
+            nc.vector.tensor_tensor(hi[r][:], b_ps[r][:], a_sb[r], ALU.max)
+
+        def mixed(r):
+            nc.vector.scalar_tensor_tensor(score[r][:], lo[r][:], lam_c[:, r : r + 1], hi[r][:], ALU.mult, ALU.add)
+
+        def shares(r):
+            nc.vector.tensor_reduce(neg_max[r][:], score[r][:], AXIS.X, ALU.max, negate=True)
+            nc.scalar.activation(p[r][:], score[r][:], ACT.Exp, bias=neg_max[r][:], accum_out=z[r][:])
+
+        def damping(r):
+            nc.vector.reciprocal(rz[r][:], z[r][:])
+            nc.vector.tensor_reduce(run_sum[r][:], by_runs(p[r][:]), AXIS.X, ALU.add)
+            nc.vector.tensor_tensor(slope[r][:], rz[r][:], neg_shy[:, r : r + 1], ALU.mult)
+            nc.scalar.activation(k0[r][:], run_sum[r][:], ACT.Exp, scale=slope[r][:])
+
+        def slot_scaled(r):
+            nc.vector.tensor_tensor(
+                pos[r][:].rearrange("m (p c) -> m p c", c=PACK), os_ps[:].rearrange("m c p -> m p c"),
+                p[r][:].rearrange("m (p c) -> m p c", c=PACK), ALU.mult,
+            )
+
+        def damped_sum(r):
+            nc.vector.scalar_tensor_tensor(
+                damped[r][:], run_sum[r][:], 1.0, k0[r][:], ALU.mult, ALU.mult, accum_out=z2[r][:]
+            )
+            nc.vector.reciprocal(rz2[r][:], z2[r][:])
+
+        def weights(r):
+            nc.vector.scalar_tensor_tensor(
+                by_runs(w_rows[r][:]), by_runs(pos[r][:]), rz2[r][:],
+                k0[r][:].unsqueeze(2).to_broadcast([P, G, RUN]), ALU.mult, ALU.mult,
+            )
+            w_ps = bank(r, [P, 2, P], "w_ps%d" % r)
+            turn(w_rows[r][:], w_ps[:])
+            w_woven = sb.tile([P, P, PACK], BF16, align_bytes=64, name="w_woven%d" % r)
+            nc.scalar.copy(as_word_pairs(w_woven[:]), w_ps[:].rearrange("p u c -> p c u"))
+            return w_woven
+
+        smaller(0)
+        larger(0)
+        smaller(1)
+        mixed(0)
+        larger(1)
+        shares(0)
+        mixed(1)
+        shares(1)
+        damping(0)
+        slot_scaled(0)
+        damping(1)
+        damped_sum(0)
+        w_woven = [weights(0)]
+        slot_scaled(1)
+        damped_sum(1)
+        w_woven.append(weights(1))
+
+        v_first = sb.tile([P, 2, I], BF16, tag="q2_woven1", align_bytes=64)
+        v_rows = [v_first[:, 0, :], v_first[:, 1, :]]
+        for r in tiles:
+            v_rows.append(sb.tile([P, I], BF16, name="v_late%d" % r, tag="slope%d" % r, align_bytes=64)[:])
+        v_groups = ((0, 1), (2,), (3,))
+        v_woven = []
+        for h, group in enumerate(v_groups):
+            n = len(group)
+            v_ps = bank((6, 5, 7)[h], [P, n, 2, P], "v_ps%d" % h)
+            for jj, j in enumerate(group):
+                nc.scalar.activation(v_rows[j], val_rows[j][:].indirect(idx[:]), ACT.Copy)
+                turn(v_rows[j], v_ps[:, jj])
+            v_woven.append(
+                sb.tile([P, n * P, PACK], BF16, align_bytes=64, name="v_woven%d" % h, tag=("score0", "rz1", "v_woven2")[h])
+            )
+            nc.scalar.copy(
+                as_word_pairs(v_woven[h][:]).rearrange("p (j c) u -> p j c u", j=n), v_ps[:].rearrange("p j u c -> p j c u")
+            )
+
+        v_codes = sb.tile([P, E], U32, align_bytes=64, tag="pos1")
+        v_scales = sb.tile([P, E], U8, align_bytes=64)
+        w_codes = sb.tile([P, Q], U32, align_bytes=64, tag="rz21")
+        w_scales = sb.tile([P, Q], U8, align_bytes=64)
+
+        def quantize_values(h):
+            cols = slice(v_groups[h][0] * P, (v_groups[h][-1] + 1) * P)
+            quantize(v_codes[:, cols], v_scales[:, cols], v_woven[h][:])
+
+        def quantize_weights(r):
+            cols = slice(r * P, (r + 1) * P)
+            quantize(w_codes[:, cols], w_scales[:, cols], w_woven[r][:])
+
+        quantize_values(0)
+        quantize_weights(0)
+        quantize_values(1)
+        quantize_values(2)
+        quantize_weights(1)
+
+        y_codes = sb.tile([P, Q], U32, align_bytes=64)
+        y_scales = sb.tile([P, Q], U8, align_bytes=64)
+        y_rows = out_0.rearrange("(p j) q -> p j q", j=PACK)
+        y_words = out_1[0].rearrange("p c t -> p (c t)").bitcast(I32)
+
+        def result(r):
+            cols = slice(r * P, (r + 1) * P)
+            first = r * P + 1
+            n = min(P, Q - first)
+            y = sb.tile([P, PACK, P], F32, name="y%d" % r)
+            y_woven = sb.tile([P, P, PACK], BF16, align_bytes=64, name="y_woven%d" % r)
+            o_ps = []
+            for h in range(2):
+                o_ps.append(bank(((2, 3), (4, 0))[r][h], [P, 2, P], "o_ps%d%d" % (r, h)))
+                for jj in range(2):
+                    e_cols = slice((2 * h + jj) * P, (2 * h + jj + 1) * P)
+                    nc.tensor.matmul_mx(
+                        out=o_ps[h][:, jj, :], lhsT=v_codes[:, e_cols].bitcast(FP8X4), lhsT_scale=v_scales[:, e_cols],
+                        rhs=w_codes[:, cols].bitcast(FP8X4), rhs_scale=w_scales[:, cols], start=True, stop=True,
+                    )
+            for h in range(2):
+                nc.vector.tensor_tensor(
+                    carried[:, 2 * h : 2 * h + 2, first : first + n], o_ps[h][:, :, :n],
+                    memq_row[:, first : first + n].unsqueeze(1).to_broadcast([P, 2, n]), ALU.mult,
+                )
+            for h in range(2):
+                nc.vector.tensor_tensor(y[:, 2 * h : 2 * h + 2, :], o_ps[h][:], carried[:, 2 * h : 2 * h + 2, cols], ALU.subtract)
+            nc.sync.dma_start(y_rows[:, :, cols], y[:])
+            weave(nc.scalar.copy if r < QT - 1 else nc.vector.tensor_copy, y_woven[:], y[:])
+            quantize(y_codes[:, cols], y_scales[:, cols], y_woven[:])
+            nc.sync.dma_start(y_words[:, cols], y_codes[:, cols].bitcast(I32))
+
+        result(0)
+        result(1)
+        y_scale_rows = out_2[0].bitcast(I32)
+        for quad in range(4):
+            queue = nc.sync if quad % 2 == 0 else nc.scalar
+            queue.dma_start(y_scale_rows[4 * quad : 4 * quad + 4, :], y_scales[32 * quad : 32 * quad + 4, :].bitcast(I32))

@@ -21,6 +21,7 @@ G = I // RUN
 P = 128
 PACK = 4
 QT = Q // P
+LAM, SHY, OS, MEMQ, VECS = 0, 2, 4, 8, 10
 FLOPS = 2 * Q * I * D * 2 + 2 * E * Q * I
 
 
@@ -51,20 +52,16 @@ def tile_attend_twopools_crowdshy_rowchanges_pl_kernel(
         q_raw = sb.tile([P, PACK, Q], F32)
         q2_raw = sb.tile([P, PACK, Q], F32)
         note_rows = [sb.tile([P, U], F32, name="note_rows%d" % t) for t in range(PACK)]
-        val_rows = [sb.tile([P, T], F32, name="val_rows%d" % j) for j in range(PACK)]
-        lam_c = sb.tile([P, QT], F32)
-        shy_c = sb.tile([P, QT], F32)
-        os_c = sb.tile([P, PACK], F32)
-        memq_c = sb.tile([P, QT], F32)
+        val_rows = [sb.tile([P, T], F32, name="val_rows%d" % j, align_bytes=64) for j in range(PACK)]
+        vec_rows = sb.tile([P, P], F32)
         ident = sb.tile([P, P], F32)
         carried = sb.tile([P, PACK, Q], F32)
 
+        nc.vector.memset(vec_rows[:], 0.0)
         nc.gpsimd.memset(key_scales[:].bitcast(I32), 0)
         make_identity(nc, ident[:])
-        nc.vector.memset(carried[:, :, 0:1], 0.0)
+        nc.scalar.activation(carried[:, :, 0:1], vec_rows[:, 0:PACK].unsqueeze(2), ACT.Copy)
 
-        with nc.allow_non_contiguous_dma(reason="one value a query row"):
-            nc.sync.dma_start(shy_c[:], shy.rearrange("(r p) o -> p (r o)", p=P))
         nc.sync.dma_start(idx[:], offs)
         nc.sync.dma_start(key_words[:].bitcast(I32), keys_words[0].bitcast(I32))
         notes_planes = notes.rearrange("(p t) u -> t p u", t=PACK)
@@ -73,21 +70,17 @@ def tile_attend_twopools_crowdshy_rowchanges_pl_kernel(
         for quad in range(4):
             nc.sync.dma_start(key_scales[32 * quad : 32 * quad + 4, :].bitcast(I32), scale_rows[4 * quad : 4 * quad + 4, :])
         nc.sync.dma_start(idx2[:], offs2)
-        nc.sync.dma_start(note_rows[1][:], notes_planes[1])
-        nc.sync.dma_start(note_rows[2][:], notes_planes[2])
-        nc.sync.dma_start(os_c[:], slot_factor.rearrange("o (p c) -> p (o c)", p=P))
-        nc.sync.dma_start(note_rows[3][:], notes_planes[3])
-        nc.sync.dma_start(memq_c[:], memq.rearrange("o (p c) -> p (o c)", p=P))
+        for t in range(1, PACK):
+            nc.sync.dma_start(note_rows[t][:], notes_planes[t])
+        nc.sync.dma_start(vec_rows[LAM : LAM + QT, :], lam.rearrange("(r p) o -> r (p o)", p=P))
+        nc.sync.dma_start(vec_rows[SHY : SHY + QT, :], shy.rearrange("(r p) o -> r (p o)", p=P))
+        nc.sync.dma_start(vec_rows[OS : OS + PACK, :], slot_factor.rearrange("o (c p) -> (o c) p", p=P))
+        nc.sync.dma_start(vec_rows[MEMQ : MEMQ + QT, :], memq.rearrange("o (r p) -> (o r) p", p=P))
         nc.sync.dma_start(q_raw[:], query.rearrange("(p t) q -> p t q", t=PACK))
         nc.sync.dma_start(q2_raw[:], query2.rearrange("(p t) q -> p t q", t=PACK))
-        with nc.allow_non_contiguous_dma(reason="one value a query row"):
-            nc.sync.dma_start(lam_c[:], lam.rearrange("(r p) o -> p (r o)", p=P))
         vals_planes = vals.rearrange("(p j) t -> j p t", j=PACK)
         for j in range(PACK):
             nc.sync.dma_start(val_rows[j][:], vals_planes[j])
-
-        neg_shy = sb.tile([P, QT], F32)
-        nc.scalar.mul(neg_shy[:], shy_c[:], -1.0)
 
         key_words_g = sb.tile([P, I], U16, align_bytes=64)
         key_scales_g = sb.tile([P, I], U8, align_bytes=64)
@@ -103,7 +96,13 @@ def tile_attend_twopools_crowdshy_rowchanges_pl_kernel(
         nc.vector.tensor_copy(notes_g[:, 2, :], note_rows[2][:].indirect(idx2[:]))
         nc.vector.tensor_copy(notes_g[:, 3, :half], note_rows[3][:].indirect(idx2[:, : half // 16]))
         nc.scalar.activation(notes_g[:, 3, half:], note_rows[3][:].indirect(idx2[:, half // 16 :]), ACT.Copy)
-        weave(nc.vector.tensor_copy, notes_woven[:], notes_g[:])
+        halves = [slice(h * half, (h + 1) * half) for h in range(2)]
+        vec_ps = bank(5, [P, P], "vec_ps")
+        nc.tensor.transpose(vec_ps[:], vec_rows[:], ident[:])
+        vec_cols = sb.tile([P, VECS], F32, tag="note_rows2")
+        nc.vector.tensor_copy(vec_cols[:], vec_ps[:, :VECS])
+        for slots in halves:
+            weave(nc.vector.tensor_copy, notes_woven[:, slots, :], notes_g[:, :, slots])
 
         def quantized_queries(raw, r, name, codes_tag):
             woven = sb.tile([P, P, PACK], BF16, align_bytes=64, name="%s_woven%d" % (name, r))
@@ -123,26 +122,21 @@ def tile_attend_twopools_crowdshy_rowchanges_pl_kernel(
             )
             if r == 0:
                 note_codes = sb.tile([P, I], U32, align_bytes=64, tag="q_woven0")
-                quantize(note_codes[:], note_scales[:], notes_woven[:])
+                for slots in halves:
+                    quantize(note_codes[:, slots], note_scales[:, slots], notes_woven[:, slots, :])
             codes, scales = quantized_queries(q2_raw, r, "q2", "q2_codes%d" % r)
             b_ps.append(bank(2 + r, [P, I], "b_ps%d" % r))
             nc.tensor.matmul_mx(
                 out=b_ps[r][:], lhsT=codes[:].bitcast(FP8X4), lhsT_scale=scales[:],
                 rhs=note_codes[:].bitcast(FP8X4), rhs_scale=note_scales[:], start=True, stop=True,
             )
-        a_both = sb.tile([P, QT, I], F32, tag="q2_raw")
         for r in range(QT):
-            a_sb.append(a_both[:, r, :])
+            a_sb.append(sb.tile([P, I], F32, name="a_sb%d" % r, tag=("q2_raw", "a_sb1")[r])[:])
             nc.scalar.copy(a_sb[r], a_ps[r][:])
 
-        os_ps = bank(4, [P, PACK, P], "os_ps")
+        os_ps = bank(1, [P, I], "os_ps")
         for c in range(PACK):
-            nc.tensor.transpose(os_ps[:, c, :], os_c[:, c : c + 1].to_broadcast([P, P]), ident[:])
-        memq_ps = bank(5, [P, QT, P], "memq_ps")
-        for c in range(QT):
-            nc.tensor.transpose(memq_ps[:, c, :], memq_c[:, c : c + 1].to_broadcast([P, P]), ident[:])
-        memq_row = sb.tile([P, Q], F32, tag="q2_codes1", align_bytes=64)
-        nc.scalar.copy(memq_row[:].rearrange("m (p c) -> m p c", c=QT), memq_ps[:].rearrange("m c p -> m p c"))
+            nc.tensor.transpose(os_ps[:, c * P : (c + 1) * P], vec_cols[:, OS + c : OS + c + 1].to_broadcast([P, P]), ident[:])
 
         def turn(rows_bf16, bank_part):
             words = rows_bf16.bitcast(F32)
@@ -169,6 +163,9 @@ def tile_attend_twopools_crowdshy_rowchanges_pl_kernel(
         def by_runs(ap):
             return ap.rearrange("p (g m) -> p g m", m=RUN)
 
+        def dealt(ap):
+            return ap.rearrange("p (s u e) -> p u s e", u=2, e=2)
+
         def smaller(r):
             nc.vector.tensor_tensor(lo[r][:], b_ps[r][:], a_sb[r], ALU.min)
 
@@ -176,7 +173,7 @@ def tile_attend_twopools_crowdshy_rowchanges_pl_kernel(
             nc.vector.tensor_tensor(hi[r][:], b_ps[r][:], a_sb[r], ALU.max)
 
         def mixed(r):
-            nc.vector.scalar_tensor_tensor(score[r][:], lo[r][:], lam_c[:, r : r + 1], hi[r][:], ALU.mult, ALU.add)
+            nc.vector.scalar_tensor_tensor(score[r][:], lo[r][:], vec_cols[:, LAM + r : LAM + r + 1], hi[r][:], ALU.mult, ALU.add)
 
         def shares(r):
             nc.vector.tensor_reduce(neg_max[r][:], score[r][:], AXIS.X, ALU.max, negate=True)
@@ -185,13 +182,12 @@ def tile_attend_twopools_crowdshy_rowchanges_pl_kernel(
         def damping(r):
             nc.vector.reciprocal(rz[r][:], z[r][:])
             nc.vector.tensor_reduce(run_sum[r][:], by_runs(p[r][:]), AXIS.X, ALU.add)
-            nc.vector.tensor_tensor(slope[r][:], rz[r][:], neg_shy[:, r : r + 1], ALU.mult)
+            nc.vector.tensor_scalar(slope[r][:], rz[r][:], vec_cols[:, SHY + r : SHY + r + 1], -1.0, ALU.mult, ALU.mult)
             nc.scalar.activation(k0[r][:], run_sum[r][:], ACT.Exp, scale=slope[r][:])
 
         def slot_scaled(r):
             nc.vector.tensor_tensor(
-                pos[r][:].rearrange("m (p c) -> m p c", c=PACK), os_ps[:].rearrange("m c p -> m p c"),
-                p[r][:].rearrange("m (p c) -> m p c", c=PACK), ALU.mult,
+                pos[r][:].rearrange("p (u s e) -> p u s e", u=2, e=2), dealt(os_ps[:]), dealt(p[r][:]), ALU.mult
             )
 
         def damped_sum(r):
@@ -201,18 +197,21 @@ def tile_attend_twopools_crowdshy_rowchanges_pl_kernel(
             nc.vector.reciprocal(rz2[r][:], z2[r][:])
 
         def weights(r):
-            nc.vector.scalar_tensor_tensor(
-                by_runs(w_rows[r][:]), by_runs(pos[r][:]), rz2[r][:],
-                k0[r][:].unsqueeze(2).to_broadcast([P, G, RUN]), ALU.mult, ALU.mult,
-            )
-            w_ps = bank(r, [P, 2, P], "w_ps%d" % r)
-            turn(w_rows[r][:], w_ps[:])
-            w_woven = sb.tile([P, P, PACK], BF16, align_bytes=64, name="w_woven%d" % r)
-            nc.scalar.copy(as_word_pairs(w_woven[:]), w_ps[:].rearrange("p u c -> p c u"))
-            return w_woven
+            w_ps = bank((0, 4)[r], [P, 2, P], "w_ps%d" % r)
+            for u in range(2):
+                part = slice(u * half, (u + 1) * half)
+                nc.vector.scalar_tensor_tensor(
+                    w_rows[r][:, part].rearrange("p (g m) -> p g m", g=G), pos[r][:, part].rearrange("p (g m) -> p g m", g=G),
+                    rz2[r][:], k0[r][:].unsqueeze(2).to_broadcast([P, G, RUN // 2]), ALU.mult, ALU.mult,
+                )
+                nc.tensor.transpose(w_ps[:, u, :], w_rows[r][:, part].bitcast(F32), ident[:])
+            return w_ps
 
         smaller(0)
         larger(0)
+        memq_ps = bank(2, [P, Q], "memq_ps")
+        for r in range(QT):
+            nc.tensor.transpose(memq_ps[:, r * P : (r + 1) * P], vec_cols[:, MEMQ + r : MEMQ + r + 1].to_broadcast([P, P]), ident[:])
         smaller(1)
         mixed(0)
         larger(1)
@@ -223,47 +222,60 @@ def tile_attend_twopools_crowdshy_rowchanges_pl_kernel(
         slot_scaled(0)
         damping(1)
         damped_sum(0)
-        w_woven = [weights(0)]
+        w_ps = [weights(0)]
         slot_scaled(1)
         damped_sum(1)
-        w_woven.append(weights(1))
+        w_ps.append(weights(1))
 
-        v_first = sb.tile([P, 2, I], BF16, tag="q2_woven1", align_bytes=64)
+        v_first = sb.tile([P, 2, I], BF16, tag="q2_codes1", align_bytes=64)
         v_rows = [v_first[:, 0, :], v_first[:, 1, :]]
         for r in tiles:
             v_rows.append(sb.tile([P, I], BF16, name="v_late%d" % r, tag="slope%d" % r, align_bytes=64)[:])
         v_groups = ((0, 1), (2,), (3,))
-        v_woven = []
+        v_ps = []
         for h, group in enumerate(v_groups):
-            n = len(group)
-            v_ps = bank((6, 5, 7)[h], [P, n, 2, P], "v_ps%d" % h)
+            v_ps.append(bank((6, 7, 3)[h], [P, len(group), 2, P], "v_ps%d" % h))
             for jj, j in enumerate(group):
                 nc.scalar.activation(v_rows[j], val_rows[j][:].indirect(idx[:]), ACT.Copy)
-                turn(v_rows[j], v_ps[:, jj])
-            v_woven.append(
-                sb.tile([P, n * P, PACK], BF16, align_bytes=64, name="v_woven%d" % h, tag=("score0", "rz1", "v_woven2")[h])
-            )
-            nc.scalar.copy(
-                as_word_pairs(v_woven[h][:]).rearrange("p (j c) u -> p j c u", j=n), v_ps[:].rearrange("p j u c -> p j c u")
-            )
+                turn(v_rows[j], v_ps[h][:, jj])
 
-        v_codes = sb.tile([P, E], U32, align_bytes=64, tag="pos1")
+        memq_row = sb.tile([P, Q], F32, tag="val_rows2", align_bytes=64)
+        nc.scalar.copy(memq_row[:], memq_ps[:])
+
+        def unload(woven, turned):
+            n = turned.shape[1]
+            nc.scalar.copy(as_word_pairs(woven).rearrange("p (j c) u -> p j c u", j=n), turned.rearrange("p j u c -> p j c u"))
+
+        early_woven = sb.tile([P, 2 * P, PACK], BF16, align_bytes=64, tag="score0")
+        middle_woven = sb.tile([P, 2 * P, PACK], BF16, align_bytes=64, tag="val_rows3")
+        late_woven = sb.tile([P, 2 * P, PACK], BF16, align_bytes=64)
+        v_woven = [early_woven[:, :P, :], early_woven[:, P:, :], middle_woven[:, :P, :], late_woven[:, :P, :]]
+        w_woven = [middle_woven[:, P:, :], late_woven[:, P:, :]]
+        unload(early_woven[:], v_ps[0][:])
+        unload(w_woven[0], w_ps[0][:].unsqueeze(1))
+        unload(v_woven[2], v_ps[1][:])
+        unload(v_woven[3], v_ps[2][:])
+        unload(w_woven[1], w_ps[1][:].unsqueeze(1))
+
+        early_codes = sb.tile([P, 2 * P], U32, align_bytes=64, tag="rz1")
+        late_codes = sb.tile([P, 2 * P], U32, align_bytes=64, tag="pos1")
+        v_codes = [early_codes[:, :P], early_codes[:, P:], late_codes[:, :P], late_codes[:, P:]]
         v_scales = sb.tile([P, E], U8, align_bytes=64)
         w_codes = sb.tile([P, Q], U32, align_bytes=64, tag="rz21")
         w_scales = sb.tile([P, Q], U8, align_bytes=64)
 
-        def quantize_values(h):
-            cols = slice(v_groups[h][0] * P, (v_groups[h][-1] + 1) * P)
-            quantize(v_codes[:, cols], v_scales[:, cols], v_woven[h][:])
+        def quantize_values(j):
+            quantize(v_codes[j], v_scales[:, j * P : (j + 1) * P], v_woven[j])
 
         def quantize_weights(r):
             cols = slice(r * P, (r + 1) * P)
-            quantize(w_codes[:, cols], w_scales[:, cols], w_woven[r][:])
+            quantize(w_codes[:, cols], w_scales[:, cols], w_woven[r])
 
         quantize_values(0)
-        quantize_weights(0)
         quantize_values(1)
+        quantize_weights(0)
         quantize_values(2)
+        quantize_values(3)
         quantize_weights(1)
 
         y_codes = sb.tile([P, Q], U32, align_bytes=64)
@@ -279,11 +291,11 @@ def tile_attend_twopools_crowdshy_rowchanges_pl_kernel(
             y_woven = sb.tile([P, P, PACK], BF16, align_bytes=64, name="y_woven%d" % r)
             o_ps = []
             for h in range(2):
-                o_ps.append(bank(((2, 3), (4, 0))[r][h], [P, 2, P], "o_ps%d%d" % (r, h)))
+                o_ps.append(bank(((2, 6), (1, 0))[r][h], [P, 2, P], "o_ps%d%d" % (r, h)))
                 for jj in range(2):
                     e_cols = slice((2 * h + jj) * P, (2 * h + jj + 1) * P)
                     nc.tensor.matmul_mx(
-                        out=o_ps[h][:, jj, :], lhsT=v_codes[:, e_cols].bitcast(FP8X4), lhsT_scale=v_scales[:, e_cols],
+                        out=o_ps[h][:, jj, :], lhsT=v_codes[2 * h + jj].bitcast(FP8X4), lhsT_scale=v_scales[:, e_cols],
                         rhs=w_codes[:, cols].bitcast(FP8X4), rhs_scale=w_scales[:, cols], start=True, stop=True,
                     )
             for h in range(2):

@@ -63,20 +63,20 @@ def tile_attend_twopools_crowdshy_rowchanges_pl_kernel(
         nc.scalar.activation(carried[:, :, 0:1], vec_rows[:, 0:PACK].unsqueeze(2), ACT.Copy)
 
         nc.sync.dma_start(idx[:], offs)
+        nc.sync.dma_start(idx2[:], offs2)
         nc.sync.dma_start(key_words[:].bitcast(I32), keys_words[0].bitcast(I32))
         notes_planes = notes.rearrange("(p t) u -> t p u", t=PACK)
         nc.sync.dma_start(note_rows[0][:], notes_planes[0])
         scale_rows = keys_scales[0].bitcast(I32)
-        for quad in range(4):
-            nc.sync.dma_start(key_scales[32 * quad : 32 * quad + 4, :].bitcast(I32), scale_rows[4 * quad : 4 * quad + 4, :])
-        nc.sync.dma_start(idx2[:], offs2)
+        for row in range(4):
+            nc.sync.dma_start(key_scales[row::32, :].bitcast(I32), scale_rows[row::4, :])
         for t in range(1, PACK):
             nc.sync.dma_start(note_rows[t][:], notes_planes[t])
+        nc.sync.dma_start(q_raw[:], query.rearrange("(p t) q -> p t q", t=PACK))
         nc.sync.dma_start(vec_rows[LAM : LAM + QT, :], lam.rearrange("(r p) o -> r (p o)", p=P))
         nc.sync.dma_start(vec_rows[SHY : SHY + QT, :], shy.rearrange("(r p) o -> r (p o)", p=P))
         nc.sync.dma_start(vec_rows[OS : OS + PACK, :], slot_factor.rearrange("o (c p) -> (o c) p", p=P))
         nc.sync.dma_start(vec_rows[MEMQ : MEMQ + QT, :], memq.rearrange("o (r p) -> (o r) p", p=P))
-        nc.sync.dma_start(q_raw[:], query.rearrange("(p t) q -> p t q", t=PACK))
         nc.sync.dma_start(q2_raw[:], query2.rearrange("(p t) q -> p t q", t=PACK))
         vals_planes = vals.rearrange("(p j) t -> j p t", j=PACK)
         for j in range(PACK):
@@ -97,12 +97,11 @@ def tile_attend_twopools_crowdshy_rowchanges_pl_kernel(
         nc.vector.tensor_copy(notes_g[:, 3, :half], note_rows[3][:].indirect(idx2[:, : half // 16]))
         nc.scalar.activation(notes_g[:, 3, half:], note_rows[3][:].indirect(idx2[:, half // 16 :]), ACT.Copy)
         halves = [slice(h * half, (h + 1) * half) for h in range(2)]
-        vec_ps = bank(5, [P, P], "vec_ps")
-        nc.tensor.transpose(vec_ps[:], vec_rows[:], ident[:])
-        vec_cols = sb.tile([P, VECS], F32, tag="note_rows2")
-        nc.vector.tensor_copy(vec_cols[:], vec_ps[:, :VECS])
         for slots in halves:
             weave(nc.vector.tensor_copy, notes_woven[:, slots, :], notes_g[:, :, slots])
+
+        vec_ps = bank(5, [P, P], "vec_ps")
+        nc.tensor.transpose(vec_ps[:], vec_rows[:], ident[:])
 
         def quantized_queries(raw, r, name, codes_tag):
             woven = sb.tile([P, P, PACK], BF16, align_bytes=64, name="%s_woven%d" % (name, r))
@@ -133,6 +132,9 @@ def tile_attend_twopools_crowdshy_rowchanges_pl_kernel(
         for r in range(QT):
             a_sb.append(sb.tile([P, I], F32, name="a_sb%d" % r, tag=("q2_raw", "a_sb1")[r])[:])
             nc.scalar.copy(a_sb[r], a_ps[r][:])
+
+        vec_cols = sb.tile([P, VECS], F32, tag="q2_woven1", align_bytes=64)
+        nc.vector.tensor_copy(vec_cols[:], vec_ps[:, :VECS])
 
         os_ps = bank(1, [P, I], "os_ps")
         for c in range(PACK):
@@ -244,7 +246,10 @@ def tile_attend_twopools_crowdshy_rowchanges_pl_kernel(
 
         def unload(woven, turned):
             n = turned.shape[1]
-            nc.scalar.copy(as_word_pairs(woven).rearrange("p (j c) u -> p j c u", j=n), turned.rearrange("p j u c -> p j c u"))
+            nc.scalar.copy(
+                as_word_pairs(woven).rearrange("p (j c i) u -> p j c u i", j=n, i=2),
+                turned.rearrange("p j u (c i) -> p j c u i", i=2),
+            )
 
         early_woven = sb.tile([P, 2 * P, PACK], BF16, align_bytes=64, tag="score0")
         middle_woven = sb.tile([P, 2 * P, PACK], BF16, align_bytes=64, tag="val_rows3")
@@ -315,4 +320,4 @@ def tile_attend_twopools_crowdshy_rowchanges_pl_kernel(
         y_scale_rows = out_2[0].bitcast(I32)
         for quad in range(4):
             queue = nc.sync if quad % 2 == 0 else nc.scalar
-            queue.dma_start(y_scale_rows[4 * quad : 4 * quad + 4, :], y_scales[32 * quad : 32 * quad + 4, :].bitcast(I32))
+            queue.dma_start(y_scale_rows[quad::4, :], y_scales[quad::32, :].bitcast(I32))

@@ -63,20 +63,20 @@ def tile_attend_twopools_crowdshy_rowchanges_pl_kernel(
         nc.scalar.activation(carried[:, :, 0:1], vec_rows[:, 0:PACK].unsqueeze(2), ACT.Copy)
 
         nc.sync.dma_start(idx[:], offs)
-        nc.sync.dma_start(idx2[:], offs2)
         nc.sync.dma_start(key_words[:].bitcast(I32), keys_words[0].bitcast(I32))
         notes_planes = notes.rearrange("(p t) u -> t p u", t=PACK)
         nc.sync.dma_start(note_rows[0][:], notes_planes[0])
         scale_rows = keys_scales[0].bitcast(I32)
-        for row in range(4):
-            nc.sync.dma_start(key_scales[row::32, :].bitcast(I32), scale_rows[row::4, :])
+        for quad in range(4):
+            nc.sync.dma_start(key_scales[32 * quad : 32 * quad + 4, :].bitcast(I32), scale_rows[4 * quad : 4 * quad + 4, :])
+        nc.sync.dma_start(idx2[:], offs2)
         for t in range(1, PACK):
             nc.sync.dma_start(note_rows[t][:], notes_planes[t])
-        nc.sync.dma_start(q_raw[:], query.rearrange("(p t) q -> p t q", t=PACK))
         nc.sync.dma_start(vec_rows[LAM : LAM + QT, :], lam.rearrange("(r p) o -> r (p o)", p=P))
         nc.sync.dma_start(vec_rows[SHY : SHY + QT, :], shy.rearrange("(r p) o -> r (p o)", p=P))
         nc.sync.dma_start(vec_rows[OS : OS + PACK, :], slot_factor.rearrange("o (c p) -> (o c) p", p=P))
         nc.sync.dma_start(vec_rows[MEMQ : MEMQ + QT, :], memq.rearrange("o (r p) -> (o r) p", p=P))
+        nc.sync.dma_start(q_raw[:], query.rearrange("(p t) q -> p t q", t=PACK))
         nc.sync.dma_start(q2_raw[:], query2.rearrange("(p t) q -> p t q", t=PACK))
         vals_planes = vals.rearrange("(p j) t -> j p t", j=PACK)
         for j in range(PACK):
@@ -97,11 +97,12 @@ def tile_attend_twopools_crowdshy_rowchanges_pl_kernel(
         nc.vector.tensor_copy(notes_g[:, 3, :half], note_rows[3][:].indirect(idx2[:, : half // 16]))
         nc.scalar.activation(notes_g[:, 3, half:], note_rows[3][:].indirect(idx2[:, half // 16 :]), ACT.Copy)
         halves = [slice(h * half, (h + 1) * half) for h in range(2)]
-        for slots in halves:
-            weave(nc.vector.tensor_copy, notes_woven[:, slots, :], notes_g[:, :, slots])
-
         vec_ps = bank(5, [P, P], "vec_ps")
         nc.tensor.transpose(vec_ps[:], vec_rows[:], ident[:])
+        vec_cols = sb.tile([P, VECS], F32, tag="note_rows2")
+        nc.vector.tensor_copy(vec_cols[:], vec_ps[:, :VECS])
+        for slots in halves:
+            weave(nc.vector.tensor_copy, notes_woven[:, slots, :], notes_g[:, :, slots])
 
         def quantized_queries(raw, r, name, codes_tag):
             woven = sb.tile([P, P, PACK], BF16, align_bytes=64, name="%s_woven%d" % (name, r))
@@ -132,9 +133,6 @@ def tile_attend_twopools_crowdshy_rowchanges_pl_kernel(
         for r in range(QT):
             a_sb.append(sb.tile([P, I], F32, name="a_sb%d" % r, tag=("q2_raw", "a_sb1")[r])[:])
             nc.scalar.copy(a_sb[r], a_ps[r][:])
-
-        vec_cols = sb.tile([P, VECS], F32, tag="q2_woven1", align_bytes=64)
-        nc.vector.tensor_copy(vec_cols[:], vec_ps[:, :VECS])
 
         os_ps = bank(1, [P, I], "os_ps")
         for c in range(PACK):
@@ -241,46 +239,40 @@ def tile_attend_twopools_crowdshy_rowchanges_pl_kernel(
                 nc.scalar.activation(v_rows[j], val_rows[j][:].indirect(idx[:]), ACT.Copy)
                 turn(v_rows[j], v_ps[h][:, jj])
 
-        memq_row = sb.tile([P, Q], F32, tag="val_rows2", align_bytes=64)
-        nc.scalar.copy(memq_row[:], memq_ps[:])
-
         def unload(woven, turned):
             n = turned.shape[1]
-            nc.scalar.copy(
-                as_word_pairs(woven).rearrange("p (j c i) u -> p j c u i", j=n, i=2),
-                turned.rearrange("p j u (c i) -> p j c u i", i=2),
-            )
+            nc.scalar.copy(as_word_pairs(woven).rearrange("p (j c) u -> p j c u", j=n), turned.rearrange("p j u c -> p j c u"))
 
         early_woven = sb.tile([P, 2 * P, PACK], BF16, align_bytes=64, tag="score0")
         middle_woven = sb.tile([P, 2 * P, PACK], BF16, align_bytes=64, tag="val_rows3")
         late_woven = sb.tile([P, 2 * P, PACK], BF16, align_bytes=64)
-        v_woven = [early_woven[:, :P, :], early_woven[:, P:, :], middle_woven[:, :P, :], late_woven[:, :P, :]]
+        v_woven = [early_woven[:], middle_woven[:, :P, :], late_woven[:, :P, :]]
         w_woven = [middle_woven[:, P:, :], late_woven[:, P:, :]]
-        unload(early_woven[:], v_ps[0][:])
+        unload(v_woven[0], v_ps[0][:])
         unload(w_woven[0], w_ps[0][:].unsqueeze(1))
-        unload(v_woven[2], v_ps[1][:])
-        unload(v_woven[3], v_ps[2][:])
+        unload(v_woven[1], v_ps[1][:])
+        memq_row = sb.tile([P, Q], F32, tag="p1", align_bytes=64)
+        nc.scalar.copy(memq_row[:], memq_ps[:])
+        unload(v_woven[2], v_ps[2][:])
         unload(w_woven[1], w_ps[1][:].unsqueeze(1))
 
-        early_codes = sb.tile([P, 2 * P], U32, align_bytes=64, tag="rz1")
-        late_codes = sb.tile([P, 2 * P], U32, align_bytes=64, tag="pos1")
-        v_codes = [early_codes[:, :P], early_codes[:, P:], late_codes[:, :P], late_codes[:, P:]]
+        v_codes = sb.tile([P, E], U32, align_bytes=64, tag="pos1")
         v_scales = sb.tile([P, E], U8, align_bytes=64)
         w_codes = sb.tile([P, Q], U32, align_bytes=64, tag="rz21")
         w_scales = sb.tile([P, Q], U8, align_bytes=64)
 
-        def quantize_values(j):
-            quantize(v_codes[j], v_scales[:, j * P : (j + 1) * P], v_woven[j])
+        def quantize_values(h):
+            cols = slice(v_groups[h][0] * P, (v_groups[h][-1] + 1) * P)
+            quantize(v_codes[:, cols], v_scales[:, cols], v_woven[h])
 
         def quantize_weights(r):
             cols = slice(r * P, (r + 1) * P)
             quantize(w_codes[:, cols], w_scales[:, cols], w_woven[r])
 
         quantize_values(0)
-        quantize_values(1)
         quantize_weights(0)
+        quantize_values(1)
         quantize_values(2)
-        quantize_values(3)
         quantize_weights(1)
 
         y_codes = sb.tile([P, Q], U32, align_bytes=64)
@@ -300,7 +292,7 @@ def tile_attend_twopools_crowdshy_rowchanges_pl_kernel(
                 for jj in range(2):
                     e_cols = slice((2 * h + jj) * P, (2 * h + jj + 1) * P)
                     nc.tensor.matmul_mx(
-                        out=o_ps[h][:, jj, :], lhsT=v_codes[2 * h + jj].bitcast(FP8X4), lhsT_scale=v_scales[:, e_cols],
+                        out=o_ps[h][:, jj, :], lhsT=v_codes[:, e_cols].bitcast(FP8X4), lhsT_scale=v_scales[:, e_cols],
                         rhs=w_codes[:, cols].bitcast(FP8X4), rhs_scale=w_scales[:, cols], start=True, stop=True,
                     )
             for h in range(2):
@@ -320,4 +312,4 @@ def tile_attend_twopools_crowdshy_rowchanges_pl_kernel(
         y_scale_rows = out_2[0].bitcast(I32)
         for quad in range(4):
             queue = nc.sync if quad % 2 == 0 else nc.scalar
-            queue.dma_start(y_scale_rows[quad::4, :], y_scales[quad::32, :].bitcast(I32))
+            queue.dma_start(y_scale_rows[4 * quad : 4 * quad + 4, :], y_scales[32 * quad : 32 * quad + 4, :].bitcast(I32))

@@ -57,8 +57,8 @@ def tile_attend_twopools_crowdshy_rowchanges_pl_kernel(
         ident = sb.tile([P, P], F32)
         carried = sb.tile([P, PACK, Q], F32)
 
+        nc.vector.memset(key_scales[:].bitcast(I32), 0)
         nc.vector.memset(vec_rows[:], 0.0)
-        nc.gpsimd.memset(key_scales[:].bitcast(I32), 0)
         make_identity(nc, ident[:])
         nc.scalar.activation(carried[:, :, 0:1], vec_rows[:, 0:PACK].unsqueeze(2), ACT.Copy)
 

from contextlib import ExitStack

import concourse.mybir as mybir
from concourse.masks import make_identity

F32 = mybir.dt.float32
BF16 = mybir.dt.bfloat16
I32 = mybir.dt.int32
U32 = mybir.dt.uint32
U16 = mybir.dt.uint16
U8 = mybir.dt.uint8
FP8X4 = mybir.dt.float8_e4m3fn_x4
FP4X4 = mybir.dt.float4_e2m1fn_x4
ALU = mybir.AluOpType
ACT = mybir.ActivationFunctionType
AXIS = mybir.AxisListType

D, T, I, Q, E, U = 512, 2048, 512, 256, 512, 1024
RUN = 8
G = I // RUN
P = 128
PACK = 4
QT = Q // P
LAM, SHY, OS, MEMQ, VECS = 0, 2, 4, 8, 10
FLOPS = 2 * Q * I * D * 2 + 2 * E * Q * I


def weave(engine_copy, dst, src):
    engine_copy(out=dst.rearrange("p (c i) t -> p c t i", i=4), in_=src.rearrange("p t (c i) -> p c t i", i=4))


def tile_attend_twopools_crowdshy_rowchanges_pl_kernel(
    tc, query, keys_words, keys_scales, query2, notes, lam, shy, slot_factor, vals, memq, offs, offs2, out_0, out_1, out_2
):
    nc = tc.nc
    with ExitStack() as ctx:
        lists = ctx.enter_context(tc.tile_pool(name="lists", bufs=1))
        sb = ctx.enter_context(tc.tile_pool(name="sb", bufs=1))
        ps = ctx.enter_context(tc.psum_pool(name="ps", bufs=1))

        def bank(n, shape, name):
            return ps.tile(shape, F32, tag="bank%d" % n, name=name)

        def quantize(codes, scales, woven):
            nc.vector.quantize_mx(out=codes.bitcast(FP8X4), scales=scales, in_=woven.rearrange("p c t -> p (c t)"))

        idx = lists.tile([P, I // 16], U16)
        idx2 = lists.tile([P, I // 16], U16)

        key_words = sb.tile([P, T], U16, align_bytes=64)
        key_scales = sb.tile([P, T], U8, align_bytes=64)
        q_raw = sb.tile([P, PACK, Q], F32)
        q2_raw = sb.tile([P, PACK, Q], F32)
        note_rows = [sb.tile([P, U], F32, name="note_rows%d" % t) for t in range(PACK)]
        val_rows = [sb.tile([P, T], F32, name="val_rows%d" % j, align_bytes=64) for j in range(PACK)]
        vec_rows = sb.tile([P, P], F32)
        ident = sb.tile([P, P], F32)
        carried = sb.tile([P, PACK, Q], F32)

        nc.vector.memset(key_scales[:].bitcast(I32), 0)
        nc.vector.memset(vec_rows[:], 0.0)
        make_identity(nc, ident[:])
        nc.scalar.activation(carried[:, :, 0:1], vec_rows[:, 0:PACK].unsqueeze(2), ACT.Copy)

        nc.sync.dma_start(idx[:], offs)
        nc.sync.dma_start(key_words[:].bitcast(I32), keys_words[0].bitcast(I32))
        notes_planes = notes.rearrange("(p t) u -> t p u", t=PACK)
        nc.sync.dma_start(note_rows[0][:], notes_planes[0])
        scale_rows = keys_scales[0].bitcast(I32)
        for quad in range(4):
            nc.sync.dma_start(key_scales[32 * quad : 32 * quad + 4, :].bitcast(I32), scale_rows[4 * quad : 4 * quad + 4, :])
        nc.sync.dma_start(idx2[:], offs2)
        for t in range(1, PACK):
            nc.sync.dma_start(note_rows[t][:], notes_planes[t])
        nc.sync.dma_start(vec_rows[LAM : LAM + QT, :], lam.rearrange("(r p) o -> r (p o)", p=P))
        nc.sync.dma_start(vec_rows[SHY : SHY + QT, :], shy.rearrange("(r p) o -> r (p o)", p=P))
        nc.sync.dma_start(vec_rows[OS : OS + PACK, :], slot_factor.rearrange("o (c p) -> (o c) p", p=P))
        nc.sync.dma_start(vec_rows[MEMQ : MEMQ + QT, :], memq.rearrange("o (r p) -> (o r) p", p=P))
        nc.sync.dma_start(q_raw[:], query.rearrange("(p t) q -> p t q", t=PACK))
        nc.sync.dma_start(q2_raw[:], query2.rearrange("(p t) q -> p t q", t=PACK))
        vals_planes = vals.rearrange("(p j) t -> j p t", j=PACK)
        for j in range(PACK):
            nc.sync.dma_start(val_rows[j][:], vals_planes[j])

        key_words_g = sb.tile([P, I], U16, align_bytes=64)
        key_scales_g = sb.tile([P, I], U8, align_bytes=64)
        nc.vector.tensor_copy(key_words_g[:], key_words[:].indirect(idx[:]))
        nc.vector.tensor_copy(key_scales_g[:], key_scales[:].indirect(idx[:]))

        notes_woven = sb.tile([P, I, PACK], BF16, align_bytes=64)
        note_scales = sb.tile([P, I], U8, align_bytes=64)
        notes_g = sb.tile([P, PACK, I], BF16)
        half = I // 2
        nc.scalar.activation(notes_g[:, 0, :], note_rows[0][:].indirect(idx2[:]), ACT.Copy)
        nc.scalar.activation(notes_g[:, 1, :], note_rows[1][:].indirect(idx2[:]), ACT.Copy)
        nc.vector.tensor_copy(notes_g[:, 2, :], note_rows[2][:].indirect(idx2[:]))
        nc.vector.tensor_copy(notes_g[:, 3, :half], note_rows[3][:].indirect(idx2[:, : half // 16]))
        nc.scalar.activation(notes_g[:, 3, half:], note_rows[3][:].indirect(idx2[:, half // 16 :]), ACT.Copy)
        halves = [slice(h * half, (h + 1) * half) for h in range(2)]
        vec_ps = bank(5, [P, P], "vec_ps")
        nc.tensor.transpose(vec_ps[:], vec_rows[:], ident[:])
        vec_cols = sb.tile([P, VECS], F32, tag="note_rows2")
        nc.vector.tensor_copy(vec_cols[:], vec_ps[:, :VECS])
        for slots in halves:
            weave(nc.vector.tensor_copy, notes_woven[:, slots, :], notes_g[:, :, slots])

        def quantized_queries(raw, r, name, codes_tag):
            woven = sb.tile([P, P, PACK], BF16, align_bytes=64, name="%s_woven%d" % (name, r))
            codes = sb.tile([P, P], U32, align_bytes=64, name="%s_codes%d" % (name, r), tag=codes_tag)
            scales = sb.tile([P, P], U8, align_bytes=64, name="%s_scales%d" % (name, r))
            weave(nc.scalar.copy, woven[:], raw[:, :, r * P : (r + 1) * P])
            quantize(codes[:], scales[:], woven[:])
            return codes, scales

        a_ps, a_sb, b_ps = [], [], []
        for r in range(QT):
            codes, scales = quantized_queries(q_raw, r, "q", ("q_codes0", "q2_woven0")[r])
            a_ps.append(bank(r, [P, I], "a_ps%d" % r))
            nc.tensor.matmul_mx(
                out=a_ps[r][:], lhsT=codes[:].bitcast(FP8X4), lhsT_scale=scales[:],
                rhs=key_words_g[:].bitcast(FP4X4), rhs_scale=key_scales_g[:], start=True, stop=True,
            )
            if r == 0:
                note_codes = sb.tile([P, I], U32, align_bytes=64, tag="q_woven0")
                for slots in halves:
                    quantize(note_codes[:, slots], note_scales[:, slots], notes_woven[:, slots, :])
            codes, scales = quantized_queries(q2_raw, r, "q2", "q2_codes%d" % r)
            b_ps.append(bank(2 + r, [P, I], "b_ps%d" % r))
            nc.tensor.matmul_mx(
                out=b_ps[r][:], lhsT=codes[:].bitcast(FP8X4), lhsT_scale=scales[:],
                rhs=note_codes[:].bitcast(FP8X4), rhs_scale=note_scales[:], start=True, stop=True,
            )
        for r in range(QT):
            a_sb.append(sb.tile([P, I], F32, name="a_sb%d" % r, tag=("q2_raw", "a_sb1")[r])[:])
            nc.scalar.copy(a_sb[r], a_ps[r][:])

        os_ps = bank(1, [P, I], "os_ps")
        for c in range(PACK):
            nc.tensor.transpose(os_ps[:, c * P : (c + 1) * P], vec_cols[:, OS + c : OS + c + 1].to_broadcast([P, P]), ident[:])

        def turn(rows_bf16, bank_part):
            words = rows_bf16.bitcast(F32)
            for u in range(2):
                nc.tensor.transpose(bank_part[:, u, :], words[:, u::2], ident[:])

        def as_word_pairs(woven):
            return woven.rearrange("p c t -> p (c t)").bitcast(F32).rearrange("p (c u) -> p c u", u=2)

        def wide(name, r, dtype=F32):
            return sb.tile([P, I], dtype, name="%s%d" % (name, r), align_bytes=64)

        def small(name, r, width=1):
            return sb.tile([P, width], F32, name="%s%d" % (name, r), align_bytes=64)

        tiles = range(QT)
        lo, hi, score, p, pos = ([wide(name, r) for r in tiles] for name in ("lo", "hi", "score", "p", "pos"))
        w_rows = [wide("w_rows", r, BF16) for r in tiles]
        neg_max, z, rz, slope, z2, rz2 = (
            [small(name, r) for r in tiles] for name in ("neg_max", "z", "rz", "slope", "z2", "rz2")
        )
        run_sum, k0, damped = ([small(name, r, G) for r in tiles] for name in ("run_sum", "k0", "damped"))

        def by_runs(ap):
            return ap.rearrange("p (g m) -> p g m", m=RUN)

        def dealt(ap):
            return ap.rearrange("p (s u e) -> p u s e", u=2, e=2)

        def smaller(r):
            nc.vector.tensor_tensor(lo[r][:], b_ps[r][:], a_sb[r], ALU.min)

        def larger(r):
            nc.vector.tensor_tensor(hi[r][:], b_ps[r][:], a_sb[r], ALU.max)

        def mixed(r):
            nc.vector.scalar_tensor_tensor(score[r][:], lo[r][:], vec_cols[:, LAM + r : LAM + r + 1], hi[r][:], ALU.mult, ALU.add)

        def shares(r):
            nc.vector.tensor_reduce(neg_max[r][:], score[r][:], AXIS.X, ALU.max, negate=True)
            nc.scalar.activation(p[r][:], score[r][:], ACT.Exp, bias=neg_max[r][:], accum_out=z[r][:])

        def damping(r):
            nc.vector.reciprocal(rz[r][:], z[r][:])
            nc.vector.tensor_reduce(run_sum[r][:], by_runs(p[r][:]), AXIS.X, ALU.add)
            nc.vector.tensor_scalar(slope[r][:], rz[r][:], vec_cols[:, SHY + r : SHY + r + 1], -1.0, ALU.mult, ALU.mult)
            nc.scalar.activation(k0[r][:], run_sum[r][:], ACT.Exp, scale=slope[r][:])

        def slot_scaled(r):
            nc.vector.tensor_tensor(
                pos[r][:].rearrange("p (u s e) -> p u s e", u=2, e=2), dealt(os_ps[:]), dealt(p[r][:]), ALU.mult
            )

        def damped_sum(r):
            nc.vector.scalar_tensor_tensor(
                damped[r][:], run_sum[r][:], 1.0, k0[r][:], ALU.mult, ALU.mult, accum_out=z2[r][:]
            )
            nc.vector.reciprocal(rz2[r][:], z2[r][:])

        def weights(r):
            w_ps = bank((0, 4)[r], [P, 2, P], "w_ps%d" % r)
            for u in range(2):
                part = slice(u * half, (u + 1) * half)
                nc.vector.scalar_tensor_tensor(
                    w_rows[r][:, part].rearrange("p (g m) -> p g m", g=G), pos[r][:, part].rearrange("p (g m) -> p g m", g=G),
                    rz2[r][:], k0[r][:].unsqueeze(2).to_broadcast([P, G, RUN // 2]), ALU.mult, ALU.mult,
                )
                nc.tensor.transpose(w_ps[:, u, :], w_rows[r][:, part].bitcast(F32), ident[:])
            return w_ps

        smaller(0)
        larger(0)
        memq_ps = bank(2, [P, Q], "memq_ps")
        for r in range(QT):
            nc.tensor.transpose(memq_ps[:, r * P : (r + 1) * P], vec_cols[:, MEMQ + r : MEMQ + r + 1].to_broadcast([P, P]), ident[:])
        smaller(1)
        mixed(0)
        larger(1)
        shares(0)
        mixed(1)
        shares(1)
        damping(0)
        slot_scaled(0)
        damping(1)
        damped_sum(0)
        w_ps = [weights(0)]
        slot_scaled(1)
        damped_sum(1)
        w_ps.append(weights(1))

        v_first = sb.tile([P, 2, I], BF16, tag="q2_codes1", align_bytes=64)
        v_rows = [v_first[:, 0, :], v_first[:, 1, :]]
        for r in tiles:
            v_rows.append(sb.tile([P, I], BF16, name="v_late%d" % r, tag="slope%d" % r, align_bytes=64)[:])
        v_groups = ((0, 1), (2,), (3,))
        v_ps = []
        for h, group in enumerate(v_groups):
            v_ps.append(bank((6, 7, 3)[h], [P, len(group), 2, P], "v_ps%d" % h))
            for jj, j in enumerate(group):
                nc.scalar.activation(v_rows[j], val_rows[j][:].indirect(idx[:]), ACT.Copy)
                turn(v_rows[j], v_ps[h][:, jj])

        def unload(woven, turned):
            n = turned.shape[1]
            nc.scalar.copy(as_word_pairs(woven).rearrange("p (j c) u -> p j c u", j=n), turned.rearrange("p j u c -> p j c u"))

        early_woven = sb.tile([P, 2 * P, PACK], BF16, align_bytes=64, tag="score0")
        middle_woven = sb.tile([P, 2 * P, PACK], BF16, align_bytes=64, tag="val_rows3")
        late_woven = sb.tile([P, 2 * P, PACK], BF16, align_bytes=64)
        v_woven = [early_woven[:], middle_woven[:, :P, :], late_woven[:, :P, :]]
        w_woven = [middle_woven[:, P:, :], late_woven[:, P:, :]]
        unload(v_woven[0], v_ps[0][:])
        unload(w_woven[0], w_ps[0][:].unsqueeze(1))
        unload(v_woven[1], v_ps[1][:])
        memq_row = sb.tile([P, Q], F32, tag="p1", align_bytes=64)
        nc.scalar.copy(memq_row[:], memq_ps[:])
        unload(v_woven[2], v_ps[2][:])
        unload(w_woven[1], w_ps[1][:].unsqueeze(1))

        v_codes = sb.tile([P, E], U32, align_bytes=64, tag="pos1")
        v_scales = sb.tile([P, E], U8, align_bytes=64)
        w_codes = sb.tile([P, Q], U32, align_bytes=64, tag="rz21")
        w_scales = sb.tile([P, Q], U8, align_bytes=64)

        def quantize_values(h):
            cols = slice(v_groups[h][0] * P, (v_groups[h][-1] + 1) * P)
            quantize(v_codes[:, cols], v_scales[:, cols], v_woven[h])

        def quantize_weights(r):
            cols = slice(r * P, (r + 1) * P)
            quantize(w_codes[:, cols], w_scales[:, cols], w_woven[r])

        quantize_values(0)
        quantize_weights(0)
        quantize_values(1)
        quantize_values(2)
        quantize_weights(1)

        y_codes = sb.tile([P, Q], U32, align_bytes=64)
        y_scales = sb.tile([P, Q], U8, align_bytes=64)
        y_rows = out_0.rearrange("(p j) q -> p j q", j=PACK)
        y_words = out_1[0].rearrange("p c t -> p (c t)").bitcast(I32)

        def result(r):
            cols = slice(r * P, (r + 1) * P)
            first = r * P + 1
            n = min(P, Q - first)
            y = sb.tile([P, PACK, P], F32, name="y%d" % r)
            y_woven = sb.tile([P, P, PACK], BF16, align_bytes=64, name="y_woven%d" % r)
            o_ps = []
            for h in range(2):
                o_ps.append(bank(((2, 6), (1, 0))[r][h], [P, 2, P], "o_ps%d%d" % (r, h)))
                for jj in range(2):
                    e_cols = slice((2 * h + jj) * P, (2 * h + jj + 1) * P)
                    nc.tensor.matmul_mx(
                        out=o_ps[h][:, jj, :], lhsT=v_codes[:, e_cols].bitcast(FP8X4), lhsT_scale=v_scales[:, e_cols],
                        rhs=w_codes[:, cols].bitcast(FP8X4), rhs_scale=w_scales[:, cols], start=True, stop=True,
                    )
            for h in range(2):
                nc.vector.tensor_tensor(
                    carried[:, 2 * h : 2 * h + 2, first : first + n], o_ps[h][:, :, :n],
                    memq_row[:, first : first + n].unsqueeze(1).to_broadcast([P, 2, n]), ALU.mult,
                )
            for h in range(2):
                nc.vector.tensor_tensor(y[:, 2 * h : 2 * h + 2, :], o_ps[h][:], carried[:, 2 * h : 2 * h + 2, cols], ALU.subtract)
            nc.sync.dma_start(y_rows[:, :, cols], y[:])
            weave(nc.scalar.copy if r < QT - 1 else nc.vector.tensor_copy, y_woven[:], y[:])
            quantize(y_codes[:, cols], y_scales[:, cols], y_woven[:])
            nc.sync.dma_start(y_words[:, cols], y_codes[:, cols].bitcast(I32))

        result(0)
        result(1)
        y_scale_rows = out_2[0].bitcast(I32)
        for quad in range(4):
            queue = nc.sync if quad % 2 == 0 else nc.scalar
            queue.dma_start(y_scale_rows[4 * quad : 4 * quad + 4, :], y_scales[32 * quad : 32 * quad + 4, :].bitcast(I32))
